import numpy as np, ml_dtypes
CORES = [1,5,17,21,33,37,49,53]
N = 8
BF = ml_dtypes.bfloat16
def f(rng, *shape):
    return (rng.standard_normal(shape, dtype=np.float32) * np.exp2(rng.integers(-2, 3, shape[:-1] + (1,)))).astype(BF)
def wide(rng, *shape):
    v = f(rng, *shape).astype(np.float32); k = shape[:-2] + (1, shape[-1])
    return (v * np.exp2(rng.integers(-6, 7, k)) * (rng.random(k) > 0.0625)).astype(BF)
def entries(a):
    return np.ascontiguousarray(a.T).reshape(-1)
def table(e):
    return np.ascontiguousarray(np.reshape(e, (-1, 16)).T).astype(np.int32)
K, V, A, R = 4096, 8192, 4096, 512
CAP, U, HS, AS = 96, 192, 3, 4
TM = 1048576
def fine(rng, v):
    return v.astype(np.float32) * (1 + rng.random(v.shape, dtype=np.float32))
def moments(rng, uneven, *shape):
    return np.floor(np.exp2(rng.random(shape) * 20)).astype(np.int64) - 1 if uneven else rng.integers(0, TM, shape)
def owners(rng, without=-1):
    return np.stack([rng.permutation(np.repeat(np.array([q for q in range(N) if q != without]), CAP))[:R] for r in range(N)])
def full(rng):
    o = []
    for r in range(N):
        a, b = (r + 1) % N, (r + 2) % N
        rest = rng.permutation(np.repeat(np.array([q for q in range(N) if q != a and q != b]), CAP))[:R - 2 * CAP]
        o.append(rng.permutation(np.concatenate([np.repeat(np.array([a, b]), CAP), rest])))
    return np.stack(o)
def make(rng, own, key, fall=True, share=False, edge=False, low=None, uneven=False):
    tt = moments(rng, uneven, N, 8, K, HS + AS)
    if fall: tt = -np.sort(-tt, axis=3)
    if low is not None: tt = tt // 2; tt[..., :HS] += TM // 2
    h = rng.integers(0, HS + 1, (N, 8, K))
    if edge: h = HS * rng.integers(0, 2, (N, 8, K)); h[:, :, :2] = HS
    ch = rng.integers(0, K, (N, 8, K)) if share else np.zeros((N, 8, K), np.int64) + np.arange(K)
    col, s = rng.integers(0, 8, (N, R)), rng.integers(0, HS + AS, (N, R)); tie = tt[own, col, ch[own, col, key], s]; u = rng.random((N, R))
    if edge: t = np.where(u < 0.2, 0, np.where(u < 0.4, TM - 1, np.where(u < 0.7, tie, np.maximum(tie - 1, 0))))
    else: t = np.where(u < 0.25, tie, moments(rng, uneven, N, R))
    if low is not None: t = np.where(low, rng.integers(0, TM // 2, (N, R)), t)
    M = min(3 * K // 4, 2 * A // (AS + 1))
    hd = np.zeros((N, 8, K), np.int32); vt = moments(rng, uneven, N, 8, V).astype(np.int32); at = moments(rng, uneven, N, 8, A).astype(np.int32)
    vp = rng.integers(0, V + A + 1, (N, 8, V)).astype(np.int32); ap = rng.integers(0, A + 1, (N, 8, A)).astype(np.int32)
    for q in range(N):
        got = own == q; kk, tk, z = key[got], t[got], (q + 1) % N
        for c in range(8):
            x = tt[q, c]; e = np.arange(HS)[:, None] < h[q, c]; no = np.cumsum(e.reshape(-1)).reshape(HS, K) - 1; e = e & (no < V); n = np.sum(e, axis=0)
            ln = rng.integers(1, AS + 1, M)
            if edge: ln = np.where(rng.integers(0, 2, M) > 0, AS, 1); ln[:2] = AS
            e2 = np.arange(AS)[:, None] < ln; no2 = np.cumsum(e2.reshape(-1)).reshape(AS, M) - 1; e2 = e2 & (no2 < A)
            sl, sl2 = rng.permutation(V), rng.permutation(A)
            if edge:
                sl, sl2 = np.arange(V), np.arange(A); sl[1], sl[V - 1] = V - 1, 1; sl2[1], sl2[A - 1] = A - 1, 1
            m = np.where(e2, sl2[np.minimum(no2, A - 1)], A)
            want = np.array([0, 1]) if edge else rng.permutation(kk[low[got]]) if low is not None else np.zeros(0, np.int64)
            p = rng.permutation(K); o = np.concatenate([want, p[~np.isin(p, want)]])[:M]
            cont = np.full(K, A); cont[o] = m[0][np.arange(M) // 2 if share else np.arange(M)]
            ci = ch[q, c][kk]; un = ~np.any((x[ci, :HS] <= tk[:, None]) & (np.arange(HS) < n[ci][:, None]), axis=1)
            w = np.bincount(ci[un], minlength=K); most = U if low is not None else int(rng.integers(U // 2, U + 1)); tot = 0
            for j in o[w[o] > 0].tolist():
                if tot + int(w[j]) <= most: tot += int(w[j])
                else: cont[j] = A
            nx = np.where(e, sl[np.minimum(no, V - 1)], V + cont)
            hd[q, c] = nx[0][ch[q, c]]; vp[q, c][nx[e]] = np.concatenate([nx[1:], (V + cont)[None]])[e]; vt[q, c][nx[e]] = x.T[:HS][e]
            ap[z, c][m[e2]] = np.concatenate([m[1:], np.full((1, M), A)])[e2]; at[z, c][m[e2]] = x[o, HS:].T[e2]
    vv, av = (fine(rng, wide(rng, N, 8, V)), fine(rng, wide(rng, N, 8, A))) if uneven else (fine(rng, f(rng, N, 8, V)), fine(rng, f(rng, N, 8, A)))
    return {"hd": hd, "vt": vt, "vp": vp, "vv": vv, "at": at, "ap": ap, "av": av, "rk": np.stack([table(own[r] * K + key[r]) for r in range(N)]), "rt": np.stack([table(t[r]) for r in range(N)])}
def setup_inputs(rng):
    return make(rng, owners(rng), rng.integers(0, K, (N, R)))
def setup_inputs_caps(rng):
    own = full(rng); key = np.zeros((N, R), np.int64)
    for q in range(N): key[own == q] = rng.permutation(K)[:np.count_nonzero(own == q)]
    far = (own - np.arange(N)[:, None]) % N
    return make(rng, own, key, low=(far == 1) | (far == 2))
def setup_inputs_few(rng):
    own = owners(rng, int(rng.integers(0, N))); pool = np.stack([rng.permutation(K)[:16] for q in range(N)])
    return make(rng, own, pool[own, rng.integers(0, 16, (N, R))])
def setup_inputs_edge(rng):
    pool = np.stack([np.concatenate([np.array([0, 1, K - 1]), 2 + rng.permutation(K - 3)[:29]]) for q in range(N)]); own = owners(rng)
    return make(rng, own, pool[own, rng.integers(0, 32, (N, R))], edge=True)
def setup_inputs_mixed(rng):
    return make(rng, owners(rng), rng.integers(0, K, (N, R)), fall=False, share=True)
def setup_inputs_spread(rng):
    return make(rng, owners(rng), rng.integers(0, K, (N, R)), uneven=True)
def check_inputs(d):
    bad = []
    for a, top in (("hd", V + A + 1), ("vt", TM), ("vp", V + A + 1), ("at", TM), ("ap", A + 1), ("rk", N * K), ("rt", TM)):
        if np.min(d[a]) < 0 or np.max(d[a]) >= top: bad.append(a + "_range")
    for a in ("vv", "av"):
        if not np.isfinite(d[a]).all(): bad.append(a + "_finite")
    if bad: return bad
    hd, vt, vp, n = d["hd"], d["vt"], d["vp"], d["hd"].astype(np.int64); ap = np.roll(d["ap"], -1, axis=0)
    for s in range(HS): n = np.where(n < V, np.take_along_axis(vp, np.minimum(n, V - 1), 2), n)
    if (n < V).any(): bad.append("chain_in_the_heap")
    n = np.maximum(n - V, 0)
    for s in range(AS): n = np.where(n < A, np.take_along_axis(ap, np.minimum(n, A - 1), 2), n)
    if (n < A).any(): bad.append("chain_in_the_archive")
    c = np.arange(8)[:, None]; un = np.zeros((N, 8), np.int64); most = 0
    for r in range(N):
        key, t = entries(d["rk"][r]), entries(d["rt"][r]); q = key // K; most = max(most, int(np.max(np.bincount(q, minlength=N)))); n = hd[q, c, key % K]
        for s in range(HS):
            i = np.minimum(n, V - 1); n = np.where(n < V, np.where(vt[q, c, i] <= t, V + A, vp[q, c, i]), n)
        for g in range(8): un[:, g] += np.bincount(q[(n[g] >= V) & (n[g] < V + A)], minlength=N)
    if most > CAP: bad.append("reads_of_a_pair")
    if np.max(un) > U: bad.append("unfinished_walks")
    return bad
def reference(hd, vt, vp, vv, at, ap, av, rk, rt):
    y = np.zeros((N, 8, R), np.float32); c = np.arange(8)[:, None]
    for r in range(N):
        key, t = entries(rk[r]), entries(rt[r]); q = key // K; z = (q + 1) % N
        n = hd[q, c, key % K]
        for s in range(HS):
            i = np.minimum(n, V - 1); hit = (n < V) & (vt[q, c, i] <= t)
            y[r] = np.where(hit, vv[q, c, i], y[r]); n = np.where(hit, V + A, np.where(n < V, vp[q, c, i], n))
        n = n - V
        for s in range(AS):
            i = np.minimum(n, A - 1); hit = (n < A) & (at[z, c, i] <= t)
            y[r] = np.where(hit, av[z, c, i], y[r]); n = np.where(hit, A, np.where(n < A, ap[z, c, i], n))
    return {"y": y}

from concourse.bass import DstId, RemoteDMATransfer
from concourse.mybir import dt, AluOpType, AxisListType, ActivationFunctionType

N, K, V, A, R = 8, 4096, 8192, 4096, 512
HW, AW = V + 8, A + 8
BIG = 2097152.0
RVP, RVT, RVV, RHD = 0, 1, 2, 3
COPY = ActivationFunctionType.Copy
ADD, MUL, MAX, MIN = AluOpType.add, AluOpType.mult, AluOpType.max, AluOpType.min
GE, GT, LT, EQ = AluOpType.is_ge, AluOpType.is_gt, AluOpType.is_lt, AluOpType.is_equal
SHR, AND = AluOpType.arith_shift_right, AluOpType.bitwise_and

SCRATCH = {}


def declare(where, dtype, **shapes):
    for n, s in shapes.items():
        SCRATCH[n] = (where, [128, s], dtype)


declare("sbuf", "float32", H=HW, AR=AW, WA=1536, ZF=512, DG=128, C8=32, M32=128, K24=24, PF=8, LB=256, RST=32, OF=4,
        KF=4, TF=4, O96=4, SC=32, UF=8, LL=512, RR=192, SND=48, RB=48, WW=20, SW=512, X0a=192, X0b=192, XT0=384, TE=48,
        QM=48, QH=96, MM=48, N4=48, SD2=96, TH=96, QA=96, QB=96, ANS=48, Y0=256, Y1=256)
declare("sbuf", "int32", RK=4, RT=4, PI=4, OI=4, KI=4, SI=4, UI=8)
declare("sbuf", "bfloat16", LTI=128, ONE=128, OH=56)
declare("sbuf", "uint16", U0=4, U1=4, OFW=32, L0=24, LST=48, AL=48)
declare("psum", "float32", px=512, psc=512, pt=512, pm=512, ph=512, pta=512, pa1=512, pa3=512)
for _k, _n in (("h", 3), ("a", 4)):
    for _i in range(1, _n + 1):
        SCRATCH["X%s%d" % (_k, _i)] = ("sbuf", [128, 776], "float32")
        for _c in (0, 1):
            SCRATCH["g%s%d%d" % (_k, _i, _c)] = ("sbuf", [128, 384], "float32")
            SCRATCH["l%s%d%d" % (_k, _i, _c)] = ("sbuf", [128, 24], "uint16")
for _n, _s in (("Dhd", [8, K]), ("Dvp", [8, V]), ("Dvt", [8, V]), ("Dap", [8, A]), ("Dat", [8, A]), ("LA", [8, 128, 6])):
    SCRATCH[_n] = ("dram", _s, "float32")
SCRATCH["OD"] = ("dram", [2, 128, 4], "uint16")
TMP = ["M1", "H1", "A1", "H2", "Q2", "PP", "P2", "T3", "H3", "A3", "M3", "B1", "B2", "E2", "N2", "F1", "F2", "F3",
       "Z2", "B3", "G1", "G2", "Z3", "T4", "B4", "E4"]
SCRATCH["tmp"] = ("sbuf", [128, 48 * len(TMP)], "float32")
SEMAPHORES = ["v", "s", "t", "gp", "ldk", "ldt", "chd", "cvp", "cvt", "cap", "cat", "ldh", "lda", "own", "od", "ow",
              "rB", "lB", "rN", "lN", "rT", "lT", "rF", "lF", "ownf", "wa0", "wa1", "st0", "st1"]


def routes(topo, cores, me):
    src, n = cores[me], len(cores)
    near, far = [], []
    for k in range(1, n):
        d = (me + k) % n
        (near if topo.chip(cores[d]) == topo.chip(src) else far).append(d)
    out, used, call, todo = [], [], 0, list(far)
    if todo:
        used = list(topo.engines(src, cores[todo[0]]))
    while todo:
        m = 1
        while m * 2 <= min(len(todo), len(used)):
            m *= 2
        per = len(used) // m
        for i in range(m):
            out.append((todo[i], used[i * per:(i + 1) * per], call))
        todo = todo[m:]
        call += 1
    for d in near:
        out.append((d, [e for e in topo.engines(src, cores[d]) if e not in used], 0))
    return out


def bits(es):
    m = 0
    for e in es:
        m |= 1 << e
    return m


def rank_program(g, core, T, topo):
    me = T.rank_of(core)
    if me is None:
        return
    cores = list(T.cores)
    prv, nxt = (me - 1) % N, (me + 1) % N
    q = {"v": g.vector, "s": g.scalar, "t": g.tensor, "y": g.sync, "g": g}
    cnt, seen = {}, {}

    def need(name, toks):
        for sem, val in toks:
            if seen.get((name, sem), 0) < val:
                q[name].wait_ge(T.sem[sem], val)
                seen[(name, sem)] = val

    def done(ins, sem, n):
        ins.then_inc(T.sem[sem], n)
        cnt[sem] = cnt.get(sem, 0) + n
        return (sem, cnt[sem])

    def tm(name):
        k = 48 * TMP.index(name)
        return T.tmp[:, k:k + 48]

    def tt(out, a, b, op, *toks):
        need("v", toks)
        return done(g.vector.tensor_tensor(out, a, b, op), "v", 1)

    def ts(out, a, s1, s2, o0, o1, *toks):
        need("v", toks)
        if o1 is None:
            return done(g.vector.tensor_scalar(out, a, s1, None, o0), "v", 1)
        return done(g.vector.tensor_scalar(out, a, s1, s2, o0, o1), "v", 1)

    def cp(out, a, *toks):
        need("v", toks)
        return done(g.vector.tensor_copy(out, a), "v", 1)

    def fill(ap, c, *toks):
        need("v", toks)
        return done(g.vector.memset(ap, c), "v", 1)

    def tr(out, a, *toks):
        need("v", toks)
        return done(g.vector.transpose(out, a), "v", 1)

    def act(out, a, *toks):
        need("s", toks)
        return done(g.scalar.activation(out, a, COPY), "s", 1)

    def mm(out, l, r, start, stop, *toks):
        need("t", toks)
        return done(g.tensor.matmul(out, l, r, start, stop), "t", 1)

    def dma(name, out, src, sem, *toks):
        need(name, toks)
        return done(q[name].dma_start(out, src), sem, 16)

    def swap(out, src, n, *toks):
        tk = None
        for gs in range(2):
            for G in range(2):
                k = 256 * gs + 128 * G
                tk = mm(out[:, gs:n:2], T.SW[:, k:k + 128], src[:, G:n:2], G == 0, G == 1, *toks)
        return tk

    def iota(out, pat, base, cm, **kw):
        return done(g.iota(out, pat, base, cm, **kw), "gp", 1)

    fl = {"allow_small_or_imprecise_dtypes": True}
    k_rk = dma("y", T.RK[:, :], T.rk[:, :], "ldk")
    k_rt = dma("s", T.RT[:, :], T.rt[:, :], "ldt")
    i_d = iota(T.DG[:, :], [[1, 128]], 0, -1, **fl)
    i_c8 = iota(T.C8[:, :], [[0, 4], [1, 8]], 0, 0, **fl)
    i_pi = iota(T.PI[:, 0:1], [[1, 1]], 0, 1)
    i_m = iota(T.M32[:, :], [[0, 4], [1, 32]], 0, 0, **fl)
    i_k = iota(T.K24[:, :], [[1, 24]], 0, 0, **fl)
    c_hd = dma("g", T.Dhd[:, :], T.hd[:, :], "chd")
    c_vp = dma("g", T.Dvp[:, :], T.vp[:, :], "cvp")
    c_vt = dma("g", T.Dvt[:, :], T.vt[:, :], "cvt")

    f0 = fill(T.ZF[:, :], 0.0)
    fill(T.H[:, V:HW], 8192.0)
    z1 = fill(T.ONE[:, :], 1.0)
    z2 = fill(T.OH[:, 0:24], 0.0)
    ts(T.LB[:, 0:128], T.DG[:, :], 0.0, None, GT, None, i_d)
    w = ts(T.LB[:, 128:256], T.DG[:, :], 0.0, 1024.0, EQ, MUL)
    k_lti = tt(T.LTI[:, :], T.LB[:, 0:128], T.LB[:, 128:256], ADD, w)
    ts(T.RST[:, :], T.C8[:, :], 0.0, None, GT, None, i_c8)
    ts(T.PI[:, 1:2], T.PI[:, 0:1], 7, None, AND, None, i_pi)
    w = ts(T.PI[:, 2:3], T.PI[:, 0:1], 4, 1, SHR, AND)
    w = cp(T.PF[:, 0:2], T.PI[:, 1:3], w)
    k_bg = ts(T.PF[:, 2:3], T.PF[:, 0:1], float(RVT), BIG, EQ, MUL, w)
    k_g0 = ts(T.PF[:, 3:4], T.PF[:, 1:2], -1.0, 1.0, MUL, ADD)
    ts(T.H[:, V:HW], T.H[:, V:HW], T.PF[:, 2:3], None, ADD, None, k_bg)
    f1 = fill(T.H[:, 0:1536], 0.0)
    for a0 in range(1536, V, 512):
        s_hi = act(T.H[:, a0:a0 + 512], T.ZF[:, :], f0)
        if a0 == 3584:
            s_lo = s_hi

    w = ts(T.OI[:, :], T.RK[:, :], 12, None, SHR, None, k_rk)
    k_of = cp(T.OF[:, :], T.OI[:, :], w)
    for f in range(4):
        k_oh = ts(T.OH[:, 24 + 8 * f:32 + 8 * f], T.C8[:, 0:8], T.OF[:, f:f + 1], None, EQ, None, k_of, z2)
    m = mm(T.px[:, 0:32], T.LTI[:, :], T.OH[:, 24:56], True, False, k_lti, k_oh)
    for d in (1, 2, 3):
        m = mm(T.px[:, 0:32], T.ONE[:, :], T.OH[:, 24 - 8 * d:56 - 8 * d], False, d == 3, z1)
    w = ts(T.KI[:, :], T.RK[:, :], 4095, None, AND, None)
    cp(T.KF[:, :], T.KI[:, :], w)
    ts(T.TF[:, :], T.RT[:, :], 1.0, None, ADD, None, k_rt)
    k_o96 = ts(T.O96[:, :], T.OF[:, :], 96.0, -1024.0, MUL, ADD)
    need("v", [m, k_o96])
    w = done(g.vector.tensor_tensor_scan(T.SC[:, :], T.RST[:, :], T.px[:, 0:32], 0.0, MUL, MAX), "v", 1)
    w = tt(T.SI[:, :], T.SC[:, 7:32:8], T.O96[:, :], ADD, w)
    ts(T.UI[:, 0:4], T.SI[:, :], 31, None, AND, None, w)
    w = ts(T.UI[:, 4:8], T.SI[:, :], 5, None, SHR, None)
    k_uf = cp(T.UF[:, :], T.UI[:, :], w)
    for f in range(4):
        ts(T.LL[:, 128 * f:128 * f + 128], T.M32[:, :], T.UF[:, f:f + 1], None, EQ, None, k_uf, i_m)
        ts(T.RR[:, 48 * f:48 * f + 48:2], T.K24[:, :], T.UF[:, 4 + f:5 + f], T.KF[:, f:f + 1], EQ, MUL, i_k)
        w = ts(T.RR[:, 48 * f + 1:48 * f + 48:2], T.K24[:, :], T.UF[:, 4 + f:5 + f], T.TF[:, f:f + 1], EQ, MUL)
        m = mm(T.psc[:, 0:48], T.LL[:, 128 * f:128 * f + 128], T.RR[:, 48 * f:48 * f + 48], f == 0, f == 3, w)
    k_snd = cp(T.SND[:, :], T.psc[:, 0:48], m)

    mine = routes(topo, cores, me)

    def spread(src, dst, rsem, lsem, tok):
        need("g", [tok])
        tot = 0
        for call in range(1 + max(c for _, _, c in mine)):
            trs = []
            for d, es, c in mine:
                if c == call:
                    rid, pid, _ = topo.addr(cores[d])
                    trs.append(RemoteDMATransfer(dst_ids=[DstId(rid=rid, pnc=pid)], dma_engine_mask=bits(es), alu_op=0,
                                                 remote_sem=T.sem[rsem], srcs=[src[:, 6 * d:6 * d + 6]], dsts=[dst]))
                    tot += len(es)
            g.remote_dma_fused(trs, local_sem=T.sem[lsem])
        return (lsem, tot)

    into = sum(len(es) for r in range(N) if r != me for d, es, _ in routes(topo, cores, r) if d == me)
    l_b = spread(T.SND, T.RB[:, 6 * me:6 * me + 6], "rB", "lB", k_snd)
    c_ap = dma("g", T.Dap[:, :], T.ap[:, :], "cap")
    c_at = dma("g", T.Dat[:, :], T["at"][:, :], "cat")

    def rows(win, lo, hi, src, row, sem, *toks):
        for gam in range(2):
            for cl in range(2):
                k = dma("y", win[16 * gam + row + 8 * cl:128:32, lo:hi], src[cl:8:2, lo:hi], sem, *toks)
        return k

    half = V // 2
    rows(T.H, 0, half, T.vv, RVV, "ldh", f1, s_lo)
    rows(T.H, 0, K, T.Dhd, RHD, "ldh", c_hd)
    rows(T.H, 0, half, T.Dvp, RVP, "ldh", c_vp)
    rows(T.H, 0, half, T.Dvt, RVT, "ldh", c_vt)
    k_own = dma("y", T.RB[:, 6 * me:6 * me + 6], T.SND[:, 6 * me:6 * me + 6], "own", k_snd)
    rows(T.H, half, V, T.vv, RVV, "ldh", s_hi)
    rows(T.H, half, V, T.Dvp, RVP, "ldh")
    k_h = rows(T.H, half, V, T.Dvt, RVT, "ldh")

    for gs in range(2):
        for G in range(2):
            k = 256 * gs + 128 * G
            col = T.PF[:, 1:2] if gs else T.PF[:, 3:4]
            k_sw = ts(T.SW[:, k:k + 128], T.DG[:, :], 16.0 * (G - gs), col, EQ, MUL, k_g0)
    ts(T.WW[:, 0:4], T.UF[:, 0:4], 6.0, None, MUL, None, k_uf)
    ts(T.WW[:, 4:8], T.UF[:, 4:8], 2.0, None, MUL, None)
    w = ts(T.WW[:, 8:12], T.OF[:, :], 186.0, None, MUL, None)
    w = tt(T.WW[:, 12:16], T.WW[:, 0:4], T.WW[:, 4:8], ADD, w)
    w = tt(T.WW[:, 16:20], T.WW[:, 12:16], T.WW[:, 8:12], ADD, w)
    ts(T.U0[:, :], T.WW[:, 16:20], 0.0, None, ADD, None, w)
    k_u = ts(T.U1[:, :], T.WW[:, 16:20], 1.0, None, ADD, None)
    w = fill(T.AR[:, A:AW], 4096.0)
    a_e = ts(T.AR[:, A:AW], T.AR[:, A:AW], T.PF[:, 2:3], None, ADD, None, w)
    a_f = fill(T.AR[:, 0:2048], 0.0)
    for b in range(2048, A, 512):
        a_s = act(T.AR[:, b:b + 512], T.ZF[:, :])
    for b in range(0, 1536, 512):
        k_w1 = act(T.WA[:, b:b + 512], T.ZF[:, :])

    dma("y", T.OD[0], T.U0[:, :], "od", k_u)
    k_od = dma("y", T.OD[1], T.U1[:, :], "od")
    for gr in range(8):
        k_ow = dma("y", T.OFW[16 * gr:16 * gr + 16, :], T.OD[gr % 2], "ow", k_od)
    rows(T.AR, 0, A, T.av, RVV, "lda", a_f, a_s)
    rows(T.AR, 0, A, T.Dap, RVP, "lda", c_ap)
    k_ar = rows(T.AR, 0, A, T.Dat, RVT, "lda", c_at)

    def row(x, r, cl=None):
        a = 8 + r + (384 * cl if cl else 0)
        return x[:, a:a + (753 if cl is None else 369):16]

    def both(x, cl):
        return x[:, 24 * cl:24 * cl + 24]

    def hd_row(cl):
        return T.XT0[:, RHD + 8 * cl:RHD + 8 * cl + 369:16]

    k_l0 = cp(T.L0[:, :], T.RB[:, 0:48:2], ("rB", into), k_own)
    win = T.H[:, 0:HW]
    need("v", [k_l0, k_h, s_hi])
    g0 = done(g.vector.tensor_copy(T.X0a[:, :], win.indirect(T.L0[:, 0:12])), "v", 1)
    g1 = act(T.X0b[:, :], win.indirect(T.L0[:, 12:24]), k_l0, k_h, s_hi)
    cp(T.TE[:, 0:24], T.RB[:, 1:48:2])
    k_te = cp(T.TE[:, 24:48], T.RB[:, 1:48:2])
    k_pt = swap(T.pt, T.TE, 48, k_te, k_sw)
    tr(T.XT0[:, 0:192], T.X0a[:, :], g0)
    w = tr(T.XT0[:, 192:384], T.X0b[:, :], g1)
    lst = [ts(T["lh1%d" % cl][:, :], hd_row(cl), float(V), None, MIN, None, w) for cl in range(2)]
    X = {}

    def walk(kind, i, offs, toks, extra, cap, mid=None):
        x = X[i] = T["X%s%d" % (kind, i)]
        new, k = [], None
        for cl in range(2):
            buf = T["g%s%d%d" % (kind, i, cl)]
            a = act(buf[:, :], win.indirect(offs[cl]), toks[cl], *extra)
            o = 384 if cl else 8
            k = tr(x[:, o:o + 384], buf[:, :], *([a] + ([k] if k else [])))
            if cap:
                new.append(ts(T["l%s%d%d" % (kind, i + 1, cl)][:, :], row(x, RVP, cl), cap, None, MIN, None, k))
            elif mid and not cl:
                mid()
        return x, k, new

    def offs(kind, i):
        return [T["l%s%d%d" % (kind, i, cl)][:, 0:24] for cl in range(2)]

    x, k1, lst = walk("h", 1, offs("h", 1), lst, [k_h], float(V))
    tt(tm("M1"), row(x, RVT), T.TE[:, :], GE, k1, k_te)
    w = tt(tm("H1"), row(x, RVT), T.TE[:, :], LT)
    tt(tm("A1"), tm("H1"), row(x, RVV), MUL, w)
    x, k2, lst = walk("h", 2, offs("h", 2), lst, [], float(V))
    for cl in range(2):
        w = tt(both(T.QM, cl), hd_row(cl), row(x, RVP, cl), MAX, k2)
    k_pm = swap(T.pm, T.QM, 48, w)
    tt(T.QH[:, 0:48], row(x, RVT), T.pt[:, 0:48], GE, k_pt)
    w = tt(tm("H2"), row(x, RVT), T.pt[:, 0:48], LT)
    w = tt(T.QH[:, 48:96], tm("H2"), row(x, RVV), MUL, w)
    k_ph = swap(T.ph, T.QH, 96, w)
    x, k3, lst = walk("h", 3, offs("h", 3), lst, [], None,
                      lambda: tt(T.MM[:, :], row(X[1], RVP), T.pm[:, 0:48], MAX, k_pm))
    w = tt(T.N4[:, :], row(x, RVP), T.MM[:, :], MAX, k3)
    k_n4 = ts(T.LST[:, :], T.N4[:, :], -float(V), None, ADD, None, w)

    zc = cores[nxt]
    rid, pid, _ = topo.addr(zc)
    es_d = topo.engines(core, zc)
    n_in = len(topo.engines(cores[prv], core))
    need("g", [k_n4])
    g.remote_dma(T.AL[:, :], T.LST[:, :], T.sem.rN, T.sem.lN, pid, rid, bits(es_d))
    tt(tm("Q2"), tm("M1"), T.ph[:, 0:48], MUL, k_ph)
    w = tt(tm("PP"), tm("M1"), T.ph[:, 48:96], MUL)
    k_t3 = tt(tm("T3"), T.TE[:, :], tm("Q2"), MUL, w)
    tt(tm("P2"), tm("PP"), tm("A1"), ADD)
    tt(tm("M3"), row(x, RVT), tm("T3"), GE, k_t3)
    w = tt(tm("H3"), row(x, RVT), tm("T3"), LT)
    tt(T.SD2[:, 0:48], tm("T3"), tm("M3"), MUL, w)
    w = tt(tm("A3"), tm("H3"), row(x, RVV), MUL)
    k_d2 = tt(T.SD2[:, 48:96], tm("P2"), tm("A3"), ADD, w)
    need("g", [k_d2])
    g.remote_dma(T.TH[:, :], T.SD2[:, :], T.sem.rT, T.sem.lT, pid, rid, bits(es_d))
    r_n, r_t = ("rN", n_in), ("rT", n_in)

    win = T.AR[:, 0:AW]
    k_pta = swap(T.pta, T.TH, 48, r_t)
    x, k1, lst = walk("a", 1, [T.AL[:, 0:24], T.AL[:, 24:48]], [r_n, r_n], [k_ar, a_e, a_s], float(A))
    x, k2, lst = walk("a", 2, offs("a", 2), lst, [], float(A))
    x1 = X[1]
    tt(T.QA[:, 0:48], row(x1, RVT), T.pta[:, 0:48], GE, k_pta)
    w = tt(tm("B1"), row(x1, RVT), T.pta[:, 0:48], LT)
    w = tt(T.QA[:, 48:96], tm("B1"), row(x1, RVV), MUL, w)
    k_pa1 = swap(T.pa1, T.QA, 96, w)
    w = tt(tm("B2"), row(x, RVT), T.TH[:, 0:48], LT, k2, r_t)
    k_e2 = tt(tm("E2"), tm("B2"), row(x, RVV), MUL, w)
    x, k3, lst = walk("a", 3, offs("a", 3), lst, [], float(A))
    tt(T.QB[:, 0:48], row(x, RVT), T.pta[:, 0:48], GE, k3)
    w = tt(tm("B3"), row(x, RVT), T.pta[:, 0:48], LT)
    w = tt(T.QB[:, 48:96], tm("B3"), row(x, RVV), MUL, w)
    k_pa3 = swap(T.pa3, T.QB, 96, w)
    tt(tm("N2"), row(X[2], RVT), T.TH[:, 0:48], GE)
    tt(tm("F1"), tm("E2"), T.pa1[:, 0:48], MUL, k_e2, k_pa1)
    w = tt(tm("F2"), T.TH[:, 48:96], T.pa1[:, 48:96], ADD)
    tt(tm("F3"), tm("F1"), tm("F2"), ADD, w)
    k_z2 = tt(tm("Z2"), tm("N2"), T.pa1[:, 0:48], MUL)
    x, k4, lst = walk("a", 4, offs("a", 4), lst, [], None)
    tt(tm("Z3"), tm("Z2"), T.pa3[:, 0:48], MUL, k_z2, k_pa3)
    w = tt(tm("G1"), tm("Z2"), T.pa3[:, 48:96], MUL)
    tt(tm("T4"), tm("Z3"), T.TH[:, 0:48], MUL, w)
    w = tt(tm("G2"), tm("G1"), tm("F3"), ADD)
    w = tt(tm("B4"), row(x, RVT), tm("T4"), LT, w, k4)
    w = tt(tm("E4"), tm("B4"), row(x, RVV), MUL, w)
    for cl in range(2):
        k_ans = tt(T.ANS[:, cl:48:2], both(tm("E4"), cl), both(tm("G2"), cl), ADD, w)

    l_f = spread(T.ANS, T.LA[prv], "rF", "lF", k_ans)
    k_of2 = dma("y", T.LA[prv], T.ANS[:, 6 * me:6 * me + 6], "ownf", k_ans)
    ends = []
    for cl, nm in ((0, "y"), (1, "s")):
        for a in range(4):
            p = 32 * a + 16 * cl
            k = dma(nm, T.WA[p:p + 1, :], T.LA[:, 32 * a:32 * a + 32, :], "wa%d" % cl, ("rF", into), k_of2, k_w1)
        ends.append(k)
    need("v", ends + [k_ow])
    yv = done(g.vector.tensor_copy(T.Y0[:, :], T.WA[:, 0:1536].indirect(T.OFW[:, 0:16])), "v", 1)
    ys = act(T.Y1[:, :], T.WA[:, 0:1536].indirect(T.OFW[:, 16:32]), *(ends + [k_ow]))
    dma("y", T.y[:, 0:256], T.Y0[0:128:16, :], "st0", yv)
    dma("s", T.y[:, 256:512], T.Y1[0:128:16, :], "st1", ys)
    need("g", [l_b, ("lN", len(es_d)), ("lT", len(es_d)), l_f, r_n, r_t, ("rF", into), ("rB", into)] + list(cnt.items()))
